import numpy as np
import ml_dtypes


def mxq(x, axis, fmt="e4m3"):
    dtype, down = {"e4m3": (ml_dtypes.float8_e4m3fn, 7), "e5m2": (ml_dtypes.float8_e5m2, 14)}[fmt]
    v = np.moveaxis(np.asarray(x, np.float32).astype(ml_dtypes.bfloat16).astype(np.float64), axis, -1)
    blocks = v.reshape(v.shape[:-1] + (-1, 32))
    amax = np.abs(blocks).max(-1, keepdims=True)
    byte = np.maximum(np.where(amax > 0, np.frexp(amax)[1] - 1 + 127, 0) - down, 1)
    scale = np.exp2(byte - 127.0)
    codes = (blocks / scale).astype(np.float32).astype(dtype).astype(np.float64)
    return np.moveaxis((codes * scale).reshape(v.shape), -1, axis)


WIDE = False


def mx_kscale(k):
    if not WIDE:
        return np.ones(k)
    levels = np.array([10, -10, 5, -5, 0])
    if k % 512:
        return np.exp2(np.random.permutation(np.resize(levels, k // 32))).repeat(32)
    a = np.empty((k // 512, 16))
    for p in range(k // 512):
        a[p, :8] = np.random.permutation(np.resize(levels, 8))
        for g in range(8):
            far = levels[np.abs(levels - a[p, g]) >= 10]
            a[p, g + 8] = far[np.random.randint(len(far))]
    return np.exp2(a.ravel()).repeat(32)


def f64(x):
    return np.asarray(x).astype(np.float64)


def striped(idx):
    return np.tile(idx.reshape(-1, 16).T, (8, 1)).astype(np.uint16)


def unstriped(offs):
    return offs[:16].T.reshape(-1).astype(np.int64)


E2M1 = np.array([0.0, 0.5, 1.0, 1.5, 2.0, 3.0, 4.0, 6.0, -0.0, -0.5, -1.0, -1.5, -2.0, -3.0, -4.0, -6.0])


def pack_weight(w, fmt):
    k, n = w.shape
    w = f64(np.asarray(w, np.float32).astype(ml_dtypes.bfloat16)).reshape(k // 32, 32, n)
    amax = np.abs(w).max(1)
    if fmt == "e4m3":
        byte = np.frexp(amax)[1] - 1 + 127 - 7
    else:
        mant, ex = np.frexp(amax / 6.0)
        byte = np.where(mant > 0.5, ex, ex - 1) + 127
    byte = np.clip(np.where(amax > 0, byte, 1), 1, 254)
    scaled = (w * np.exp2(127.0 - byte)[:, None, :]).reshape(k, n).astype(np.float32)
    by_word = np.ascontiguousarray(scaled.reshape(k // 512, 128, 4, n).transpose(0, 1, 3, 2))
    if fmt == "e4m3":
        words = by_word.astype(ml_dtypes.float8_e4m3fn).view(np.uint8)
    else:
        c = by_word.astype(ml_dtypes.float4_e2m1fn).view(np.uint8) & 0xF
        words = (c[..., 0::2] | (c[..., 1::2] << 4)).reshape(k // 512, 128, 2 * n)
    return np.ascontiguousarray(words), np.ascontiguousarray(byte.astype(np.uint8).reshape(k // 512, 16, n))


def unpack_weight(words, scales, fmt):
    g, _, n = scales.shape
    words = np.ascontiguousarray(words).reshape(g, 128, n, -1)
    if fmt == "e4m3":
        vals = words.view(ml_dtypes.float8_e4m3fn).astype(np.float64)
    else:
        nib = np.empty((g, 128, n, 4), np.uint8)
        nib[..., 0::2] = words & 0xF
        nib[..., 1::2] = words >> 4
        vals = E2M1[nib]
    vals = vals * np.repeat(np.exp2(scales.astype(np.float64) - 127.0), 8, axis=1)[..., None]
    return vals.transpose(0, 1, 3, 2).reshape(g * 512, n)


def gelu(v):
    return 0.5 * v * (1.0 + np.tanh(np.sqrt(2.0 / np.pi) * (v + 0.044715 * v**3)))


T, S, K, KA, H, T2, P = 2048, 1024, 1024, 512, 1024, 2048, 512

def setup_inputs():
    n = np.random.standard_normal
    s = mx_kscale(K)[:, None]
    u = mx_kscale(H)[:, None]
    tab_words, tab_scales = pack_weight(n((K, T)) * s, "e4m3")
    w4_words, w4_scales = pack_weight(n((KA, H)) / np.sqrt(K) / s[:KA], "e2m1")
    return {
        "tab_words": tab_words, "tab_scales": tab_scales,
        "w4_words": w4_words, "w4_scales": w4_scales,
        "w1": (n((K - KA, H)) / np.sqrt(K) / s[KA:]).astype(np.float32),
        "yields": (0.8 * n((H, S))).astype(np.float32),
        "gain": (1.2 * np.exp(0.3 * n(H)) * u[:, 0]).astype(np.float32),
        "wgs": np.exp(0.3 * n((128, S))).astype(np.float32),
        "page0": (n((H, T2)) * u).astype(np.float32),
        "floor_r": ((0.5 * n(H) - 0.2) * u[:, 0]).astype(np.float32),
        "sv": (n(H) / np.sqrt(H) / u[:, 0] ** 2).astype(np.float32),
        "gel": np.exp(0.3 * n(P)).astype(np.float32),
        "tmpl": (0.7 * n(P)).astype(np.float32),
        "offs": striped(np.random.permutation(T)[:S]),
        "offs2": striped(np.random.permutation(T2)[:S]),
        "offs3": striped(np.random.permutation(T2)[:P]),
        "offs4": striped(np.random.permutation(T2)[:P]),
    }

def reference(tab_words, tab_scales, w4_words, w4_scales, w1, yields, gain, wgs, page0, floor_r, sv, gel, tmpl, offs, offs2, offs3, offs4):
    v = unpack_weight(tab_words, tab_scales, "e4m3")[:, unstriped(offs)]
    w4 = unpack_weight(w4_words, w4_scales, "e2m1")
    d = w4.T @ v[:KA] + mxq(f64(w1), 0, "e4m3").T @ v[KA:]
    h = np.tanh(d + f64(yields)) * f64(gain)[:, None]
    page = f64(page0).copy()
    page[:, unstriped(offs2)] = np.tile(f64(wgs), (H // 128, 1)) * h
    x1 = page[:, unstriped(offs3)]
    x2 = np.maximum(page[:, unstriped(offs4)], f64(floor_r)[:, None]) * f64(sv)[:, None]
    e = mxq(x1, 0, "e4m3").T @ mxq(x2, 0, "e4m3")
    return e * f64(gel)[:, None] + f64(tmpl)[None, :]

@@ -1,0 +1,265 @@
+from contextlib import ExitStack
+
+import concourse.mybir as mybir
+from concourse.masks import make_identity
+
+T, S, K, KA, H, T2, P2 = 2048, 1024, 1024, 512, 1024, 2048, 512
+FLOPS = 2 * K * H * S + 2 * H * P2 * P2
+
+F32 = mybir.dt.float32
+BF16 = mybir.dt.bfloat16
+I32 = mybir.dt.int32
+U32 = mybir.dt.uint32
+U16 = mybir.dt.uint16
+U8 = mybir.dt.uint8
+FP8X4 = mybir.dt.float8_e4m3fn_x4
+FP4X4 = mybir.dt.float4_e2m1fn_x4
+ALU = mybir.AluOpType
+ACT = mybir.ActivationFunctionType
+
+P = 128
+PACK = 4
+PASS = P * PACK
+BANK = 512
+HALVES = S // BANK
+GROUPS = H // PASS
+TILES = GROUPS * PACK
+H_BUFS = 3
+Y_BUFS = 4
+
+
+def tile_list_gel_template_match_kernel(
+    tc, tab_words, tab_scales, w4_words, w4_scales, w1, yields, gain, wgs, page0,
+    floor_r, sv, gel, tmpl, offs, offs2, offs3, offs4, out,
+):
+    nc = tc.nc
+    with ExitStack() as ctx:
+        lists = ctx.enter_context(tc.tile_pool(name="lists", bufs=1))
+        sb = ctx.enter_context(tc.tile_pool(name="sb", bufs=1))
+        psum = ctx.enter_context(tc.psum_pool(name="psum", bufs=1))
+
+        def sbuf(shape, dtype, name, tag=None):
+            return sb.tile(shape, dtype, name=name, tag=tag or name, align_bytes=64)
+
+        def load_list(src, name):
+            tile = lists.tile(list(src.shape), U16, name=name, tag=name)
+            nc.sync.dma_start(tile[:], src)
+            return tile
+
+        def load_rows(vec, name):
+            tile = sbuf([P, GROUPS, PACK], F32, name)
+            nc.sync.dma_start(tile[:], vec.rearrange("(b p t) -> p b t", b=GROUPS, t=PACK))
+            return tile
+
+        tab_plane = sbuf([P, T], U8, "tab_plane")
+        nc.vector.memset(tab_plane[:].bitcast(I32), 0)
+        w4_plane_raw = sbuf([P, H], U8, "w4_plane_raw")
+        nc.gpsimd.memset(w4_plane_raw[:].bitcast(I32), 0)
+        for q in range(4):
+            nc.gpsimd.dma_start(
+                w4_plane_raw[32 * q : 32 * q + 4, :].bitcast(I32),
+                w4_scales[0, 4 * q : 4 * q + 4, :].bitcast(I32),
+            )
+        ident = sbuf([P, P], F32, "ident")
+        make_identity(nc, ident[:])
+
+        idx = load_list(offs, "idx")
+        w4_raw = sbuf([P, 2 * H], U8, "w4_raw")
+        nc.sync.dma_start(w4_raw[:].bitcast(I32), w4_words[0].bitcast(I32))
+
+        def load_table(a):
+            tile = sbuf([P, T], U32, "tab%d" % a)
+            nc.sync.dma_start(
+                tile[:].bitcast(I32), tab_words[a].rearrange("p t i -> p (t i)").bitcast(I32)
+            )
+            return tile
+
+        def load_w1(b):
+            tile = sbuf([P, PACK, PASS], F32, "w1_raw%d" % b)
+            nc.sync.dma_start(
+                tile[:], w1[:, b * PASS : (b + 1) * PASS].rearrange("(p j) c -> p j c", j=PACK)
+            )
+            return tile
+
+        table = [load_table(0)]
+        for q in range(4):
+            nc.sync.dma_start(
+                tab_plane[32 * q : 32 * q + 8, :].bitcast(I32),
+                tab_scales[:, 4 * q : 4 * q + 4, :].bitcast(I32),
+            )
+        w1_raw = [load_w1(0)]
+        table.append(load_table(1))
+
+        w4_codes = sbuf([P, 2 * H], U8, "w4_codes")
+        nc.vector.tensor_copy(
+            w4_codes[:].bitcast(U16).rearrange("p (b t q) -> p b t q", b=GROUPS, t=PACK),
+            w4_raw[:].bitcast(U16).rearrange("p (b q t) -> p b t q", b=GROUPS, t=PACK),
+        )
+        w4_plane = sbuf([P, H], U8, "w4_plane")
+        nc.vector.tensor_copy(
+            w4_plane[:].rearrange("p (b t q) -> p b t q", b=GROUPS, t=PACK),
+            w4_plane_raw[:].rearrange("p (b q t) -> p b t q", b=GROUPS, t=PACK),
+        )
+
+        def quantize(src, name, tag=None):
+            width = src.shape[1] // PACK
+            codes = sbuf([P, width], U32, name + "_codes", tag)
+            plane = sbuf([P, width], U8, name + "_plane")
+            nc.vector.quantize_mx(out=codes[:].bitcast(FP8X4), scales=plane[:], in_=src[:])
+            return codes, plane
+
+        def quantize_w1(b):
+            woven = sbuf([P, PASS * PACK], BF16, "w1_woven%d" % b)
+            nc.scalar.copy(
+                woven[:].rearrange("p (t m j) -> p m t j", t=PACK, j=PACK),
+                w1_raw[b][:].rearrange("p j (m t) -> p m t j", t=PACK),
+            )
+            return quantize(woven, "w1q%d" % b)
+
+        def gather_table(half):
+            cols = idx[:, half * (BANK // 16) : (half + 1) * (BANK // 16)]
+            first = sbuf([P, BANK], U32, "v0_%d" % half)
+            nc.vector.tensor_copy(first[:], table[0][:].indirect(cols))
+            plane = sbuf([P, BANK], U8, "vs_%d" % half)
+            nc.vector.tensor_copy(plane[:], tab_plane[:].indirect(cols))
+            second = sbuf([P, BANK], U32, "v1_%d" % half)
+            nc.vector.tensor_copy(second[:], table[1][:].indirect(cols))
+            return first, second, plane
+
+        w1q = [quantize_w1(0)]
+        picked = [gather_table(half) for half in range(HALVES)]
+
+        rows = "(b p t) j -> b t p j"
+        yields_rows = yields.rearrange(rows, b=GROUPS, t=PACK)
+        page_rows = page0.rearrange(rows, b=GROUPS, t=PACK)
+        wgs_rows = wgs.rearrange("(q t) j -> t q j", t=PACK)
+
+        def load_tile(i):
+            b, t = divmod(i, PACK)
+            y = sbuf([P, S], F32, "y%d" % i, "y%d" % (i % Y_BUFS))
+            nc.sync.dma_start(y[:], yields_rows[b, t])
+            if b == 0:
+                w = sbuf([P, S], F32, "wgs%d" % t)
+                for rep in range(4):
+                    nc.sync.dma_start(w[32 * rep : 32 * rep + 32, :], wgs_rows[t])
+                wgs_sb.append(w)
+            page = sbuf([P, T2], F32, "page%d" % i)
+            nc.sync.dma_start(page[:], page_rows[b, t])
+            return y, page
+
+        def features(i, half, y, h):
+            b, t = divmod(i, PACK)
+            parity = half % 2
+            first, second, plane = picked[half]
+            col = b * PASS + t * P
+            d_ps = psum.tile([P, BANK], F32, name="d_ps", tag="d%d" % parity)
+            nc.tensor.matmul_mx(
+                d_ps[:], lhsT=w4_codes[:, 2 * col : 2 * (col + P)].bitcast(FP4X4),
+                lhsT_scale=w4_plane[:, col : col + P],
+                rhs=first[:].bitcast(FP8X4), rhs_scale=plane[:], start=True, stop=False,
+            )
+            codes, scales = w1q[b]
+            nc.tensor.matmul_mx(
+                d_ps[:], lhsT=codes[:, t * P : (t + 1) * P].bitcast(FP8X4),
+                lhsT_scale=scales[:, t * P : (t + 1) * P],
+                rhs=second[:].bitcast(FP8X4), rhs_scale=plane[4:P, :], start=False, stop=True,
+            )
+            d_sb = sbuf([P, BANK], F32, "d_sb", "d_sb%d" % parity)
+            nc.scalar.copy(d_sb[:], d_ps[:])
+            sum_ps = psum.tile([P, BANK], F32, name="sum_ps", tag="s%d" % parity)
+            for c in range(4):
+                j0 = half * BANK + c * P
+                nc.tensor.matmul(
+                    sum_ps[:, c * P : (c + 1) * P], lhsT=y[:, j0 : j0 + P], rhs=ident[:],
+                    is_transpose=True, start=(c == 0), stop=False,
+                )
+            for c in range(4):
+                nc.tensor.matmul(
+                    sum_ps[:, c * P : (c + 1) * P], lhsT=d_sb[:, c * P : (c + 1) * P], rhs=ident[:],
+                    is_transpose=True, start=False, stop=(c == 3),
+                )
+            tanh_sb = sbuf([P, BANK], F32, "tanh_sb", "tanh_sb%d" % parity)
+            nc.scalar.activation(tanh_sb[:], sum_ps[:], ACT.Tanh)
+            back_ps = psum.tile([P, BANK], F32, name="back_ps", tag="z%d" % parity)
+            for c in range(4):
+                nc.tensor.transpose(
+                    back_ps[:, c * P : (c + 1) * P], tanh_sb[:, c * P : (c + 1) * P], ident[:]
+                )
+            nc.scalar.activation(
+                h[:, half * BANK : (half + 1) * BANK], back_ps[:], ACT.Copy,
+                scale=gain_sb[:, b, t : t + 1],
+            )
+
+        def weave(engine_copy, planes, name, tag=None):
+            woven = sbuf([P, P2 * PACK], BF16, name, tag)
+            engine_copy(
+                woven[:].rearrange("p (c i t) -> p c t i", i=4, t=PACK),
+                planes[:].rearrange("p t (c i) -> p c t i", i=4),
+            )
+            return woven
+
+        wgs_sb = []
+        x1_planes = [sbuf([P, PACK, P2], BF16, "x1_planes%d" % b) for b in range(GROUPS)]
+        x2_planes = [sbuf([P, PACK, P2], BF16, "x2_planes%d" % b) for b in range(GROUPS)]
+        x1q, x2q = [], []
+        for i in range(TILES):
+            b, t = divmod(i, PACK)
+            y, page = load_tile(i)
+            if i == 0:
+                idx2 = load_list(offs2, "idx2")
+                gain_sb = load_rows(gain, "gain_sb")
+                idx4 = load_list(offs4, "idx4")
+                idx3 = load_list(offs3, "idx3")
+                floor_sb = load_rows(floor_r, "floor_sb")
+                sv_sb = load_rows(sv, "sv_sb")
+            if i == 1:
+                w1_raw.append(load_w1(1))
+            if i == 2:
+                w1q.append(quantize_w1(1))
+            h = sbuf([P, S], F32, "h%d" % i, "h%d" % (i % H_BUFS))
+            for half in range(HALVES):
+                features(i, half, y, h)
+            if i == 5:
+                x1q.append(quantize(weave(nc.scalar.copy, x1_planes[0], "x1_woven0", "y1"), "x1q0", "wgs0"))
+            if i == 6:
+                x2q.append(quantize(weave(nc.scalar.copy, x2_planes[0], "x2_woven0", "y2"), "x2q0", "wgs1"))
+            pieces = HALVES if i == 0 else 1
+            width = S // pieces
+            for k in range(pieces):
+                nc.vector.tensor_tensor(
+                    page[:].indirect(idx2[:, k * width // 16 : (k + 1) * width // 16]),
+                    h[:, k * width : (k + 1) * width], wgs_sb[t][:, k * width : (k + 1) * width],
+                    ALU.mult,
+                )
+            x2_raw = sbuf([P, P2], F32, "x2_raw", "x2_raw%d" % (i % 2))
+            nc.vector.tensor_copy(x2_raw[:], page[:].indirect(idx4[:]))
+            nc.vector.tensor_copy(x1_planes[b][:, t, :], page[:].indirect(idx3[:]))
+            nc.vector.tensor_scalar(
+                x2_planes[b][:, t, :], x2_raw[:], floor_sb[:, b, t : t + 1], sv_sb[:, b, t : t + 1],
+                ALU.max, ALU.mult,
+            )
+
+        gel_sb = sbuf([P, P2 // P], F32, "gel_sb")
+        with nc.allow_non_contiguous_dma(reason="one gel factor for each partition"):
+            nc.sync.dma_start(gel_sb[:], gel.rearrange("(c p) -> p c", p=P))
+        tmpl_sb = sbuf([P, P2], F32, "tmpl_sb")
+        nc.sync.dma_start(tmpl_sb[:], tmpl.partition_broadcast(P))
+
+        x2_last = weave(nc.scalar.copy, x2_planes[1], "x2_woven1")
+        x1q.append(quantize(weave(nc.vector.tensor_copy, x1_planes[1], "x1_woven1"), "x1q1"))
+        x2q.append(quantize(x2_last, "x2q1"))
+
+        for c, tag in enumerate(("z0", "z1", "s0", "s1")):
+            e_ps = psum.tile([P, P2], F32, name="e_ps", tag=tag)
+            for b in range(GROUPS):
+                nc.tensor.matmul_mx(
+                    e_ps[:], lhsT=x1q[b][0][:, c * P : (c + 1) * P].bitcast(FP8X4),
+                    lhsT_scale=x1q[b][1][:, c * P : (c + 1) * P],
+                    rhs=x2q[b][0][:].bitcast(FP8X4), rhs_scale=x2q[b][1][:],
+                    start=(b == 0), stop=(b == GROUPS - 1),
+                )
+            result = sbuf([P, P2], F32, "result%d" % c)
+            nc.vector.scalar_tensor_tensor(
+                result[:], e_ps[:], gel_sb[:, c : c + 1], tmpl_sb[:], ALU.mult, ALU.add
+            )
+            nc.sync.dma_start(out[c * P : (c + 1) * P, :], result[:])

@@ -3,7 +3,7 @@ from contextlib import ExitStack
 import concourse.mybir as mybir
 from concourse.masks import make_identity
 
-T, S, K, KA, H, T2, P2 = 2048, 1024, 1024, 512, 1024, 2048, 512
+T, S, K, H, T2, P2 = 2048, 1024, 1024, 1024, 2048, 512
 FLOPS = 2 * K * H * S + 2 * H * P2 * P2
 
 F32 = mybir.dt.float32
@@ -20,12 +20,20 @@ ACT = mybir.ActivationFunctionType
 P = 128
 PACK = 4
 PASS = P * PACK
+QUADRANT = 32
+QUADRANTS = P // QUADRANT
+SCALE_ROWS = 4
+STRIPE = 16
 BANK = 512
 HALVES = S // BANK
+BLOCKS = BANK // P
 GROUPS = H // PASS
 TILES = GROUPS * PACK
+RUN = 4
+W1_PARTS = 2
 H_BUFS = 3
 Y_BUFS = 4
+WEAVE = 4
 
 
 def tile_list_gel_template_match_kernel(
@@ -46,26 +54,39 @@ def tile_list_gel_template_match_kernel(
             nc.sync.dma_start(tile[:], src)
             return tile
 
-        def load_rows(vec, name):
-            tile = sbuf([P, GROUPS, PACK], F32, name)
-            nc.sync.dma_start(tile[:], vec.rearrange("(b p t) -> p b t", b=GROUPS, t=PACK))
-            return tile
-
         tab_plane = sbuf([P, T], U8, "tab_plane")
         nc.vector.memset(tab_plane[:].bitcast(I32), 0)
         w4_plane_raw = sbuf([P, H], U8, "w4_plane_raw")
-        nc.gpsimd.memset(w4_plane_raw[:].bitcast(I32), 0)
-        for q in range(4):
-            nc.gpsimd.dma_start(
-                w4_plane_raw[32 * q : 32 * q + 4, :].bitcast(I32),
-                w4_scales[0, 4 * q : 4 * q + 4, :].bitcast(I32),
-            )
+        nc.vector.memset(w4_plane_raw[:].bitcast(I32), 0)
         ident = sbuf([P, P], F32, "ident")
         make_identity(nc, ident[:])
 
+        def load_vectors(queue, vectors, name):
+            raw = sbuf([len(vectors) * GROUPS, PASS], F32, name + "_raw")
+            for n, vec in enumerate(vectors):
+                queue.dma_start(
+                    raw[n * GROUPS : (n + 1) * GROUPS, :], vec.rearrange("(b r) -> b r", b=GROUPS)
+                )
+            return raw
+
+        def turn_vectors(raw, name, tag=None):
+            count = raw.shape[0]
+            dealt = sbuf([P, PASS], F32, name + "_dealt", tag)
+            nc.gpsimd.memset(dealt[:], 0.0)
+            nc.scalar.copy(
+                dealt[:count, :].rearrange("k (t g e) -> k t g e", t=PACK, e=RUN),
+                raw[:].rearrange("k (g t e) -> k t g e", t=PACK, e=RUN),
+            )
+            vec_ps = psum.tile([P, PACK, P], F32, name="vec_ps", tag="vec")
+            for t in range(PACK):
+                nc.tensor.transpose(vec_ps[:, t, :], dealt[:, t * P : (t + 1) * P], ident[:])
+            tile = sbuf([P, PACK, count], F32, name + "_sb")
+            nc.scalar.copy(tile[:], vec_ps[:, :, :count])
+            return tile
+
         idx = load_list(offs, "idx")
-        w4_raw = sbuf([P, 2 * H], U8, "w4_raw")
-        nc.sync.dma_start(w4_raw[:].bitcast(I32), w4_words[0].bitcast(I32))
+        gain_sb = turn_vectors(load_vectors(nc.sync, [gain], "gain"), "gain")
+        x2_vectors = load_vectors(nc.gpsimd, [floor_r, sv], "x2_vectors")
 
         def load_table(a):
             tile = sbuf([P, T], U32, "tab%d" % a)
@@ -75,167 +96,228 @@ def tile_list_gel_template_match_kernel(
             return tile
 
         def load_w1(b):
-            tile = sbuf([P, PACK, PASS], F32, "w1_raw%d" % b)
-            nc.sync.dma_start(
-                tile[:], w1[:, b * PASS : (b + 1) * PASS].rearrange("(p j) c -> p j c", j=PACK)
-            )
-            return tile
+            parts = []
+            for n in range(W1_PARTS):
+                width = PASS // W1_PARTS
+                tile = sbuf([P, PACK, width], F32, "w1_raw%d_%d" % (b, n))
+                c0 = b * PASS + n * width
+                nc.sync.dma_start(
+                    tile[:], w1[:, c0 : c0 + width].rearrange("(p j) c -> p j c", j=PACK)
+                )
+                parts.append(tile)
+            return parts
 
+        tab_rows = sbuf([P, T // PACK], I32, "tab_rows")
+        for q in range(QUADRANTS):
+            live = slice(QUADRANT * q, QUADRANT * q + 2 * SCALE_ROWS)
+            rows_q = tab_scales[:, SCALE_ROWS * q : SCALE_ROWS * (q + 1), :]
+            nc.sync.dma_start(tab_rows[live, :], rows_q.bitcast(I32))
+            nc.vector.tensor_copy(tab_plane[live, :].bitcast(I32), tab_rows[live, :])
         table = [load_table(0)]
-        for q in range(4):
-            nc.sync.dma_start(
-                tab_plane[32 * q : 32 * q + 8, :].bitcast(I32),
-                tab_scales[:, 4 * q : 4 * q + 4, :].bitcast(I32),
-            )
         w1_raw = [load_w1(0)]
+        w4_raw = sbuf([P, 2 * H], U8, "w4_raw")
+        nc.sync.dma_start(w4_raw[:].bitcast(I32), w4_words[0].bitcast(I32))
+        for q in range(QUADRANTS):
+            nc.sync.dma_start(
+                w4_plane_raw[QUADRANT * q : QUADRANT * q + SCALE_ROWS, :].bitcast(I32),
+                w4_scales[0, SCALE_ROWS * q : SCALE_ROWS * (q + 1), :].bitcast(I32),
+            )
         table.append(load_table(1))
 
         w4_codes = sbuf([P, 2 * H], U8, "w4_codes")
         nc.vector.tensor_copy(
-            w4_codes[:].bitcast(U16).rearrange("p (b t q) -> p b t q", b=GROUPS, t=PACK),
-            w4_raw[:].bitcast(U16).rearrange("p (b q t) -> p b t q", b=GROUPS, t=PACK),
-        )
-        w4_plane = sbuf([P, H], U8, "w4_plane")
-        nc.vector.tensor_copy(
-            w4_plane[:].rearrange("p (b t q) -> p b t q", b=GROUPS, t=PACK),
-            w4_plane_raw[:].rearrange("p (b q t) -> p b t q", b=GROUPS, t=PACK),
+            w4_codes[:].bitcast(I32).rearrange("p (b t g w) -> p b t g w", b=GROUPS, t=PACK, w=2),
+            w4_raw[:].bitcast(I32).rearrange("p (b g t w) -> p b t g w", b=GROUPS, t=PACK, w=2),
         )
 
         def quantize(src, name, tag=None):
             width = src.shape[1] // PACK
             codes = sbuf([P, width], U32, name + "_codes", tag)
             plane = sbuf([P, width], U8, name + "_plane")
-            nc.vector.quantize_mx(out=codes[:].bitcast(FP8X4), scales=plane[:], in_=src[:])
+            nc.vector.quantize_mx(out=codes[:].bitcast(FP8X4), scales=plane[:], in_=src)
             return codes, plane
 
-        def quantize_w1(b):
-            woven = sbuf([P, PASS * PACK], BF16, "w1_woven%d" % b)
-            nc.scalar.copy(
-                woven[:].rearrange("p (t m j) -> p m t j", t=PACK, j=PACK),
-                w1_raw[b][:].rearrange("p j (m t) -> p m t j", t=PACK),
-            )
-            return quantize(woven, "w1q%d" % b)
+        def quantize_w1(b, tag=None):
+            woven = sbuf([P, PASS * PACK], BF16, "w1_woven%d" % b, tag)
+            dealt = woven[:].rearrange("p (t g e j) -> p g t e j", t=PACK, e=RUN, j=PACK)
+            runs = P // RUN // W1_PARTS
+            for n, part in enumerate(w1_raw[b]):
+                nc.scalar.copy(
+                    dealt[:, n * runs : (n + 1) * runs],
+                    part[:].rearrange("p j (g t e) -> p g t e j", t=PACK, e=RUN),
+                )
+            return quantize(woven[:], "w1q%d" % b)
 
-        def gather_table(half):
-            cols = idx[:, half * (BANK // 16) : (half + 1) * (BANK // 16)]
-            first = sbuf([P, BANK], U32, "v0_%d" % half)
-            nc.vector.tensor_copy(first[:], table[0][:].indirect(cols))
-            plane = sbuf([P, BANK], U8, "vs_%d" % half)
-            nc.vector.tensor_copy(plane[:], tab_plane[:].indirect(cols))
-            second = sbuf([P, BANK], U32, "v1_%d" % half)
-            nc.vector.tensor_copy(second[:], table[1][:].indirect(cols))
-            return first, second, plane
+        def gather_halves(window, dtype, name):
+            tile = sbuf([P, S], dtype, name)
+            halves = []
+            for half in range(HALVES):
+                dst = tile[:, half * BANK : (half + 1) * BANK]
+                entries = idx[:, half * BANK // STRIPE : (half + 1) * BANK // STRIPE]
+                nc.vector.tensor_copy(dst, window[:].indirect(entries))
+                halves.append(dst)
+            return halves
 
         w1q = [quantize_w1(0)]
-        picked = [gather_table(half) for half in range(HALVES)]
+        w4_plane = sbuf([P, H], U8, "w4_plane")
+        nc.vector.tensor_copy(
+            w4_plane[:].bitcast(I32).rearrange("p (b t g) -> p b t g", b=GROUPS, t=PACK),
+            w4_plane_raw[:].bitcast(I32).rearrange("p (b g t) -> p b t g", b=GROUPS, t=PACK),
+        )
+        v_plane = gather_halves(tab_plane, U8, "v_plane")
+        v_first = gather_halves(table[0], U32, "v_first")
+        v_second = gather_halves(table[1], U32, "v_second")
 
-        rows = "(b p t) j -> b t p j"
-        yields_rows = yields.rearrange(rows, b=GROUPS, t=PACK)
-        page_rows = page0.rearrange(rows, b=GROUPS, t=PACK)
-        wgs_rows = wgs.rearrange("(q t) j -> t q j", t=PACK)
+        rows = "(b g t e) j -> b t g e j"
+        yields_rows = yields.rearrange(rows, b=GROUPS, t=PACK, e=RUN)
+        page_rows = page0.rearrange(rows, b=GROUPS, t=PACK, e=RUN)
+        wgs_rows = wgs.rearrange("(g t e) j -> t g e j", t=PACK, e=RUN)
 
-        def load_tile(i):
+        def load_wgs(t, cols):
+            for q in range(QUADRANTS):
+                nc.sync.dma_start(
+                    wgs_sb[t][QUADRANT * q : QUADRANT * (q + 1), cols], wgs_rows[t][:, :, cols]
+                )
+
+        def product(i, half):
             b, t = divmod(i, PACK)
-            y = sbuf([P, S], F32, "y%d" % i, "y%d" % (i % Y_BUFS))
-            nc.sync.dma_start(y[:], yields_rows[b, t])
-            if b == 0:
-                w = sbuf([P, S], F32, "wgs%d" % t)
-                for rep in range(4):
-                    nc.sync.dma_start(w[32 * rep : 32 * rep + 32, :], wgs_rows[t])
-                wgs_sb.append(w)
-            page = sbuf([P, T2], F32, "page%d" % i)
-            nc.sync.dma_start(page[:], page_rows[b, t])
-            return y, page
-
-        def features(i, half, y, h):
-            b, t = divmod(i, PACK)
-            parity = half % 2
-            first, second, plane = picked[half]
             col = b * PASS + t * P
-            d_ps = psum.tile([P, BANK], F32, name="d_ps", tag="d%d" % parity)
+            d_ps = psum.tile([P, BANK], F32, name="d_ps", tag="sum%d" % half)
             nc.tensor.matmul_mx(
                 d_ps[:], lhsT=w4_codes[:, 2 * col : 2 * (col + P)].bitcast(FP4X4),
                 lhsT_scale=w4_plane[:, col : col + P],
-                rhs=first[:].bitcast(FP8X4), rhs_scale=plane[:], start=True, stop=False,
+                rhs=v_first[half].bitcast(FP8X4), rhs_scale=v_plane[half],
+                start=True, stop=False,
             )
-            codes, scales = w1q[b]
+            codes, plane = w1q[b]
             nc.tensor.matmul_mx(
                 d_ps[:], lhsT=codes[:, t * P : (t + 1) * P].bitcast(FP8X4),
-                lhsT_scale=scales[:, t * P : (t + 1) * P],
-                rhs=second[:].bitcast(FP8X4), rhs_scale=plane[4:P, :], start=False, stop=True,
+                lhsT_scale=plane[:, t * P : (t + 1) * P],
+                rhs=v_second[half].bitcast(FP8X4), rhs_scale=v_plane[half][SCALE_ROWS:P, :],
+                start=False, stop=True,
             )
-            d_sb = sbuf([P, BANK], F32, "d_sb", "d_sb%d" % parity)
+            return d_ps
+
+        def features_first(half, y, h):
+            cols = slice(half * BANK, (half + 1) * BANK)
+            d_ps = product(0, half)
+            d_sb = sbuf([P, BANK], F32, "d_sb", "d_sb%d" % half)
+            nc.vector.tensor_tensor(d_sb[:], d_ps[:], y[:, cols], ALU.add)
+            tanh_sb = sbuf([P, BANK], F32, "tanh_sb", "tanh_sb0")
+            nc.scalar.activation(tanh_sb[:], d_sb[:], ACT.Tanh)
+            nc.scalar.activation(h[:, cols], tanh_sb[:], ACT.Copy, scale=gain_sb[:, 0, 0:1])
+
+        def features(i, half, y, h):
+            b, t = divmod(i, PACK)
+            j0 = half * BANK
+            d_ps = product(i, half)
+            d_sb = sbuf([P, BANK], F32, "d_sb", "d_sb%d" % half)
             nc.scalar.copy(d_sb[:], d_ps[:])
-            sum_ps = psum.tile([P, BANK], F32, name="sum_ps", tag="s%d" % parity)
-            for c in range(4):
-                j0 = half * BANK + c * P
+            sum_ps = psum.tile([P, BANK], F32, name="sum_ps", tag="sum%d" % half)
+            for c in range(BLOCKS):
                 nc.tensor.matmul(
-                    sum_ps[:, c * P : (c + 1) * P], lhsT=y[:, j0 : j0 + P], rhs=ident[:],
-                    is_transpose=True, start=(c == 0), stop=False,
+                    sum_ps[:, c * P : (c + 1) * P], lhsT=y[:, j0 + c * P : j0 + (c + 1) * P],
+                    rhs=ident[:], is_transpose=True, start=(c == 0), stop=False,
                 )
-            for c in range(4):
+            for c in range(BLOCKS):
                 nc.tensor.matmul(
                     sum_ps[:, c * P : (c + 1) * P], lhsT=d_sb[:, c * P : (c + 1) * P], rhs=ident[:],
-                    is_transpose=True, start=False, stop=(c == 3),
+                    is_transpose=True, start=False, stop=(c == BLOCKS - 1),
                 )
-            tanh_sb = sbuf([P, BANK], F32, "tanh_sb", "tanh_sb%d" % parity)
+            tanh_sb = sbuf([P, BANK], F32, "tanh_sb", "tanh_sb%d" % half)
             nc.scalar.activation(tanh_sb[:], sum_ps[:], ACT.Tanh)
-            back_ps = psum.tile([P, BANK], F32, name="back_ps", tag="z%d" % parity)
-            for c in range(4):
+            back_ps = psum.tile([P, BANK], F32, name="back_ps", tag="back%d" % half)
+            for c in range(BLOCKS):
                 nc.tensor.transpose(
                     back_ps[:, c * P : (c + 1) * P], tanh_sb[:, c * P : (c + 1) * P], ident[:]
                 )
             nc.scalar.activation(
-                h[:, half * BANK : (half + 1) * BANK], back_ps[:], ACT.Copy,
-                scale=gain_sb[:, b, t : t + 1],
+                h[:, j0 : j0 + BANK], back_ps[:], ACT.Copy, scale=gain_sb[:, t, b : b + 1]
             )
 
-        def weave(engine_copy, planes, name, tag=None):
-            woven = sbuf([P, P2 * PACK], BF16, name, tag)
-            engine_copy(
-                woven[:].rearrange("p (c i t) -> p c t i", i=4, t=PACK),
-                planes[:].rearrange("p t (c i) -> p c t i", i=4),
+        def weave(woven, places, t0, count):
+            which = slice(t0, t0 + count)
+            nc.scalar.copy(
+                woven.rearrange("p (c i t) -> p c t i", i=WEAVE, t=PACK)[:, :, which, :],
+                places[:, which, :].rearrange("p t (c i) -> p c t i", i=WEAVE),
             )
             return woven
 
-        wgs_sb = []
-        x1_planes = [sbuf([P, PACK, P2], BF16, "x1_planes%d" % b) for b in range(GROUPS)]
-        x2_planes = [sbuf([P, PACK, P2], BF16, "x2_planes%d" % b) for b in range(GROUPS)]
+        vectors_after = 0
+        w1_after = 2
+        x1_after = PACK + 1
+        x2_after = PACK + 2
+
+        wgs_sb = [sbuf([P, S], F32, "wgs%d" % t) for t in range(PACK)]
+        x1_places = [sbuf([P, PACK, P2], BF16, "x1_places%d" % b) for b in range(GROUPS)]
+        x2_places = [sbuf([P, PACK, P2], BF16, "x2_places%d" % b) for b in range(GROUPS)]
         x1q, x2q = [], []
         for i in range(TILES):
             b, t = divmod(i, PACK)
-            y, page = load_tile(i)
-            if i == 0:
+            first, last = i == 0, i == TILES - 1
+            y_tag = "y%d" % (i % Y_BUFS)
+            y = sbuf([P, S], F32, "y%d" % i, y_tag)
+            nc.sync.dma_start(y[:], yields_rows[b, t])
+            if first:
                 idx2 = load_list(offs2, "idx2")
-                gain_sb = load_rows(gain, "gain_sb")
+            page = sbuf([P, T2], F32, "page%d" % i)
+            nc.sync.dma_start(page[:], page_rows[b, t])
+            if first:
+                for half in range(HALVES):
+                    load_wgs(t, slice(half * BANK, (half + 1) * BANK))
                 idx4 = load_list(offs4, "idx4")
                 idx3 = load_list(offs3, "idx3")
-                floor_sb = load_rows(floor_r, "floor_sb")
-                sv_sb = load_rows(sv, "sv_sb")
-            if i == 1:
+            elif b == 0:
+                load_wgs(t, slice(0, S))
+            if i == w1_after - 1:
                 w1_raw.append(load_w1(1))
-            if i == 2:
-                w1q.append(quantize_w1(1))
+
             h = sbuf([P, S], F32, "h%d" % i, "h%d" % (i % H_BUFS))
             for half in range(HALVES):
-                features(i, half, y, h)
-            if i == 5:
-                x1q.append(quantize(weave(nc.scalar.copy, x1_planes[0], "x1_woven0", "y1"), "x1q0", "wgs0"))
-            if i == 6:
-                x2q.append(quantize(weave(nc.scalar.copy, x2_planes[0], "x2_woven0", "y2"), "x2q0", "wgs1"))
-            pieces = HALVES if i == 0 else 1
-            width = S // pieces
-            for k in range(pieces):
-                nc.vector.tensor_tensor(
-                    page[:].indirect(idx2[:, k * width // 16 : (k + 1) * width // 16]),
-                    h[:, k * width : (k + 1) * width], wgs_sb[t][:, k * width : (k + 1) * width],
-                    ALU.mult,
+                if first:
+                    features_first(half, y, h)
+                else:
+                    features(i, half, y, h)
+
+            if i == vectors_after:
+                x2_sb = turn_vectors(x2_vectors, "x2_vectors", y_tag)
+            if i == w1_after:
+                w1q.append(quantize_w1(1, y_tag))
+            if i == x1_after:
+                woven = sbuf([P, P2 * PACK], BF16, "x1_woven0", y_tag)
+                x1q.append(
+                    quantize(weave(woven[:], x1_places[0], 0, PACK), "x1q0", "wgs%d" % (t - 1))
                 )
-            x2_raw = sbuf([P, P2], F32, "x2_raw", "x2_raw%d" % (i % 2))
-            nc.vector.tensor_copy(x2_raw[:], page[:].indirect(idx4[:]))
-            nc.vector.tensor_copy(x1_planes[b][:, t, :], page[:].indirect(idx3[:]))
+            if i == x2_after:
+                woven = sbuf([P, P2 * PACK], BF16, "x2_woven0", y_tag)
+                x2q.append(
+                    quantize(weave(woven[:], x2_places[0], 0, PACK), "x2q0", "wgs%d" % (t - 1))
+                )
+            if last:
+                woven = sbuf([P, 2 * P2 * PACK], BF16, "woven1", "tanh_sb1")
+                x2_last = weave(woven[:, P2 * PACK :], x2_places[b], 0, PACK - 1)
+                x1_last = weave(woven[:, : P2 * PACK], x1_places[b], 0, PACK - 1)
+
+            width = BANK if first else S
+            for j0 in range(0, S, width):
+                nc.vector.tensor_tensor(
+                    page[:].indirect(idx2[:, j0 // STRIPE : (j0 + width) // STRIPE]),
+                    h[:, j0 : j0 + width], wgs_sb[t][:, j0 : j0 + width], ALU.mult,
+                )
+
+            if last:
+                nc.vector.tensor_copy(x1_places[b][:, t, :], page[:].indirect(idx3[:]))
+                weave(x1_last, x1_places[b], t, 1)
+                x2_raw = sbuf([P, P2], F32, "x2_raw", "x2_places%d" % b)
+                x2_out = x2_last.rearrange("p (c t) -> p t c", t=PACK)[:, t, :]
+                nc.vector.tensor_copy(x2_raw[:], page[:].indirect(idx4[:]))
+            else:
+                x2_raw = sbuf([P, P2], F32, "x2_raw", "x2_raw%d" % (i % 2))
+                x2_out = x2_places[b][:, t, :]
+                nc.vector.tensor_copy(x2_raw[:], page[:].indirect(idx4[:]))
+                nc.vector.tensor_copy(x1_places[b][:, t, :], page[:].indirect(idx3[:]))
             nc.vector.tensor_scalar(
-                x2_planes[b][:, t, :], x2_raw[:], floor_sb[:, b, t : t + 1], sv_sb[:, b, t : t + 1],
+                x2_out, x2_raw[:], x2_sb[:, t, b : b + 1], x2_sb[:, t, GROUPS + b : GROUPS + b + 1],
                 ALU.max, ALU.mult,
             )
 
@@ -245,12 +327,19 @@ def tile_list_gel_template_match_kernel(
         tmpl_sb = sbuf([P, P2], F32, "tmpl_sb")
         nc.sync.dma_start(tmpl_sb[:], tmpl.partition_broadcast(P))
 
-        x2_last = weave(nc.scalar.copy, x2_planes[1], "x2_woven1")
-        x1q.append(quantize(weave(nc.vector.tensor_copy, x1_planes[1], "x1_woven1"), "x1q1"))
+        x1_codes = sbuf([P, P2], U32, "x1q1_codes")
+        x1_plane = sbuf([P, P2], U8, "x1q1_plane")
+        nc.vector.quantize_mx(
+            out=x1_codes[:, :P].bitcast(FP8X4), scales=x1_plane[:, :P], in_=x1_last[:, : P * PACK]
+        )
         x2q.append(quantize(x2_last, "x2q1"))
+        nc.vector.quantize_mx(
+            out=x1_codes[:, P:].bitcast(FP8X4), scales=x1_plane[:, P:], in_=x1_last[:, P * PACK :]
+        )
+        x1q.append((x1_codes, x1_plane))
 
-        for c, tag in enumerate(("z0", "z1", "s0", "s1")):
-            e_ps = psum.tile([P, P2], F32, name="e_ps", tag=tag)
+        for c, bank in enumerate(("back0", "back1", "sum0", "sum1")):
+            e_ps = psum.tile([P, P2], F32, name="e_ps", tag=bank)
             for b in range(GROUPS):
                 nc.tensor.matmul_mx(
                     e_ps[:], lhsT=x1q[b][0][:, c * P : (c + 1) * P].bitcast(FP8X4),

from contextlib import ExitStack

import concourse.mybir as mybir
from concourse.masks import make_identity

T, S, K, H, T2, P2 = 2048, 1024, 1024, 1024, 2048, 512
FLOPS = 2 * K * H * S + 2 * H * P2 * P2

F32 = mybir.dt.float32
BF16 = mybir.dt.bfloat16
I32 = mybir.dt.int32
U32 = mybir.dt.uint32
U16 = mybir.dt.uint16
U8 = mybir.dt.uint8
FP8X4 = mybir.dt.float8_e4m3fn_x4
FP4X4 = mybir.dt.float4_e2m1fn_x4
ALU = mybir.AluOpType
ACT = mybir.ActivationFunctionType

P = 128
PACK = 4
PASS = P * PACK
QUADRANT = 32
QUADRANTS = P // QUADRANT
SCALE_ROWS = 4
STRIPE = 16
BANK = 512
HALVES = S // BANK
BLOCKS = BANK // P
GROUPS = H // PASS
TILES = GROUPS * PACK
RUN = 4
W1_PARTS = 2
H_BUFS = 3
Y_BUFS = 4
WEAVE = 4


def tile_list_gel_template_match_kernel(
    tc, tab_words, tab_scales, w4_words, w4_scales, w1, yields, gain, wgs, page0,
    floor_r, sv, gel, tmpl, offs, offs2, offs3, offs4, out,
):
    nc = tc.nc
    with ExitStack() as ctx:
        lists = ctx.enter_context(tc.tile_pool(name="lists", bufs=1))
        sb = ctx.enter_context(tc.tile_pool(name="sb", bufs=1))
        psum = ctx.enter_context(tc.psum_pool(name="psum", bufs=1))

        def sbuf(shape, dtype, name, tag=None):
            return sb.tile(shape, dtype, name=name, tag=tag or name, align_bytes=64)

        def load_list(src, name):
            tile = lists.tile(list(src.shape), U16, name=name, tag=name)
            nc.sync.dma_start(tile[:], src)
            return tile

        tab_plane = sbuf([P, T], U8, "tab_plane")
        nc.vector.memset(tab_plane[:].bitcast(I32), 0)
        w4_plane_raw = sbuf([P, H], U8, "w4_plane_raw")
        nc.vector.memset(w4_plane_raw[:].bitcast(I32), 0)
        ident = sbuf([P, P], F32, "ident")
        make_identity(nc, ident[:])

        def load_vectors(queue, vectors, name):
            raw = sbuf([len(vectors) * GROUPS, PASS], F32, name + "_raw")
            for n, vec in enumerate(vectors):
                queue.dma_start(
                    raw[n * GROUPS : (n + 1) * GROUPS, :], vec.rearrange("(b r) -> b r", b=GROUPS)
                )
            return raw

        def turn_vectors(raw, name, tag=None):
            count = raw.shape[0]
            dealt = sbuf([P, PASS], F32, name + "_dealt", tag)
            nc.gpsimd.memset(dealt[:], 0.0)
            nc.scalar.copy(
                dealt[:count, :].rearrange("k (t g e) -> k t g e", t=PACK, e=RUN),
                raw[:].rearrange("k (g t e) -> k t g e", t=PACK, e=RUN),
            )
            vec_ps = psum.tile([P, PACK, P], F32, name="vec_ps", tag="vec")
            for t in range(PACK):
                nc.tensor.transpose(vec_ps[:, t, :], dealt[:, t * P : (t + 1) * P], ident[:])
            tile = sbuf([P, PACK, count], F32, name + "_sb")
            nc.scalar.copy(tile[:], vec_ps[:, :, :count])
            return tile

        idx = load_list(offs, "idx")
        gain_sb = turn_vectors(load_vectors(nc.sync, [gain], "gain"), "gain")
        x2_vectors = load_vectors(nc.gpsimd, [floor_r, sv], "x2_vectors")

        def load_table(a):
            tile = sbuf([P, T], U32, "tab%d" % a)
            nc.sync.dma_start(
                tile[:].bitcast(I32), tab_words[a].rearrange("p t i -> p (t i)").bitcast(I32)
            )
            return tile

        def load_w1(b):
            parts = []
            for n in range(W1_PARTS):
                width = PASS // W1_PARTS
                tile = sbuf([P, PACK, width], F32, "w1_raw%d_%d" % (b, n))
                c0 = b * PASS + n * width
                nc.sync.dma_start(
                    tile[:], w1[:, c0 : c0 + width].rearrange("(p j) c -> p j c", j=PACK)
                )
                parts.append(tile)
            return parts

        tab_rows = sbuf([P, T // PACK], I32, "tab_rows")
        for q in range(QUADRANTS):
            live = slice(QUADRANT * q, QUADRANT * q + 2 * SCALE_ROWS)
            rows_q = tab_scales[:, SCALE_ROWS * q : SCALE_ROWS * (q + 1), :]
            nc.sync.dma_start(tab_rows[live, :], rows_q.bitcast(I32))
            nc.vector.tensor_copy(tab_plane[live, :].bitcast(I32), tab_rows[live, :])
        table = [load_table(0)]
        w1_raw = [load_w1(0)]
        w4_raw = sbuf([P, 2 * H], U8, "w4_raw")
        nc.sync.dma_start(w4_raw[:].bitcast(I32), w4_words[0].bitcast(I32))
        for q in range(QUADRANTS):
            nc.sync.dma_start(
                w4_plane_raw[QUADRANT * q : QUADRANT * q + SCALE_ROWS, :].bitcast(I32),
                w4_scales[0, SCALE_ROWS * q : SCALE_ROWS * (q + 1), :].bitcast(I32),
            )
        table.append(load_table(1))

        w4_codes = sbuf([P, 2 * H], U8, "w4_codes")
        nc.vector.tensor_copy(
            w4_codes[:].bitcast(I32).rearrange("p (b t g w) -> p b t g w", b=GROUPS, t=PACK, w=2),
            w4_raw[:].bitcast(I32).rearrange("p (b g t w) -> p b t g w", b=GROUPS, t=PACK, w=2),
        )

        def quantize(src, name, tag=None):
            width = src.shape[1] // PACK
            codes = sbuf([P, width], U32, name + "_codes", tag)
            plane = sbuf([P, width], U8, name + "_plane")
            nc.vector.quantize_mx(out=codes[:].bitcast(FP8X4), scales=plane[:], in_=src)
            return codes, plane

        def quantize_w1(b, tag=None):
            woven = sbuf([P, PASS * PACK], BF16, "w1_woven%d" % b, tag)
            dealt = woven[:].rearrange("p (t g e j) -> p g t e j", t=PACK, e=RUN, j=PACK)
            runs = P // RUN // W1_PARTS
            for n, part in enumerate(w1_raw[b]):
                nc.scalar.copy(
                    dealt[:, n * runs : (n + 1) * runs],
                    part[:].rearrange("p j (g t e) -> p g t e j", t=PACK, e=RUN),
                )
            return quantize(woven[:], "w1q%d" % b)

        def gather_halves(window, dtype, name):
            tile = sbuf([P, S], dtype, name)
            halves = []
            for half in range(HALVES):
                dst = tile[:, half * BANK : (half + 1) * BANK]
                entries = idx[:, half * BANK // STRIPE : (half + 1) * BANK // STRIPE]
                nc.vector.tensor_copy(dst, window[:].indirect(entries))
                halves.append(dst)
            return halves

        w1q = [quantize_w1(0)]
        w4_plane = sbuf([P, H], U8, "w4_plane")
        nc.vector.tensor_copy(
            w4_plane[:].bitcast(I32).rearrange("p (b t g) -> p b t g", b=GROUPS, t=PACK),
            w4_plane_raw[:].bitcast(I32).rearrange("p (b g t) -> p b t g", b=GROUPS, t=PACK),
        )
        v_plane = gather_halves(tab_plane, U8, "v_plane")
        v_first = gather_halves(table[0], U32, "v_first")
        v_second = gather_halves(table[1], U32, "v_second")

        rows = "(b g t e) j -> b t g e j"
        yields_rows = yields.rearrange(rows, b=GROUPS, t=PACK, e=RUN)
        page_rows = page0.rearrange(rows, b=GROUPS, t=PACK, e=RUN)
        wgs_rows = wgs.rearrange("(g t e) j -> t g e j", t=PACK, e=RUN)

        def load_wgs(t, cols):
            for q in range(QUADRANTS):
                nc.sync.dma_start(
                    wgs_sb[t][QUADRANT * q : QUADRANT * (q + 1), cols], wgs_rows[t][:, :, cols]
                )

        def product(i, half):
            b, t = divmod(i, PACK)
            col = b * PASS + t * P
            d_ps = psum.tile([P, BANK], F32, name="d_ps", tag="sum%d" % half)
            nc.tensor.matmul_mx(
                d_ps[:], lhsT=w4_codes[:, 2 * col : 2 * (col + P)].bitcast(FP4X4),
                lhsT_scale=w4_plane[:, col : col + P],
                rhs=v_first[half].bitcast(FP8X4), rhs_scale=v_plane[half],
                start=True, stop=False,
            )
            codes, plane = w1q[b]
            nc.tensor.matmul_mx(
                d_ps[:], lhsT=codes[:, t * P : (t + 1) * P].bitcast(FP8X4),
                lhsT_scale=plane[:, t * P : (t + 1) * P],
                rhs=v_second[half].bitcast(FP8X4), rhs_scale=v_plane[half][SCALE_ROWS:P, :],
                start=False, stop=True,
            )
            return d_ps

        def features_first(half, y, h):
            cols = slice(half * BANK, (half + 1) * BANK)
            d_ps = product(0, half)
            d_sb = sbuf([P, BANK], F32, "d_sb", "d_sb%d" % half)
            nc.vector.tensor_tensor(d_sb[:], d_ps[:], y[:, cols], ALU.add)
            tanh_sb = sbuf([P, BANK], F32, "tanh_sb", "tanh_sb0")
            nc.scalar.activation(tanh_sb[:], d_sb[:], ACT.Tanh)
            nc.scalar.activation(h[:, cols], tanh_sb[:], ACT.Copy, scale=gain_sb[:, 0, 0:1])

        def features(i, half, y, h):
            b, t = divmod(i, PACK)
            j0 = half * BANK
            d_ps = product(i, half)
            d_sb = sbuf([P, BANK], F32, "d_sb", "d_sb%d" % half)
            nc.scalar.copy(d_sb[:], d_ps[:])
            sum_ps = psum.tile([P, BANK], F32, name="sum_ps", tag="sum%d" % half)
            for c in range(BLOCKS):
                nc.tensor.matmul(
                    sum_ps[:, c * P : (c + 1) * P], lhsT=y[:, j0 + c * P : j0 + (c + 1) * P],
                    rhs=ident[:], is_transpose=True, start=(c == 0), stop=False,
                )
            for c in range(BLOCKS):
                nc.tensor.matmul(
                    sum_ps[:, c * P : (c + 1) * P], lhsT=d_sb[:, c * P : (c + 1) * P], rhs=ident[:],
                    is_transpose=True, start=False, stop=(c == BLOCKS - 1),
                )
            tanh_sb = sbuf([P, BANK], F32, "tanh_sb", "tanh_sb%d" % half)
            nc.scalar.activation(tanh_sb[:], sum_ps[:], ACT.Tanh)
            back_ps = psum.tile([P, BANK], F32, name="back_ps", tag="back%d" % half)
            for c in range(BLOCKS):
                nc.tensor.transpose(
                    back_ps[:, c * P : (c + 1) * P], tanh_sb[:, c * P : (c + 1) * P], ident[:]
                )
            nc.scalar.activation(
                h[:, j0 : j0 + BANK], back_ps[:], ACT.Copy, scale=gain_sb[:, t, b : b + 1]
            )

        def weave(woven, places, t0, count):
            which = slice(t0, t0 + count)
            nc.scalar.copy(
                woven.rearrange("p (c i t) -> p c t i", i=WEAVE, t=PACK)[:, :, which, :],
                places[:, which, :].rearrange("p t (c i) -> p c t i", i=WEAVE),
            )
            return woven

        vectors_after = 0
        w1_after = 2
        x1_after = PACK + 1
        x2_after = PACK + 2

        wgs_sb = [sbuf([P, S], F32, "wgs%d" % t) for t in range(PACK)]
        x1_places = [sbuf([P, PACK, P2], BF16, "x1_places%d" % b) for b in range(GROUPS)]
        x2_places = [sbuf([P, PACK, P2], BF16, "x2_places%d" % b) for b in range(GROUPS)]
        x1q, x2q = [], []
        for i in range(TILES):
            b, t = divmod(i, PACK)
            first, last = i == 0, i == TILES - 1
            y_tag = "y%d" % (i % Y_BUFS)
            y = sbuf([P, S], F32, "y%d" % i, y_tag)
            nc.sync.dma_start(y[:], yields_rows[b, t])
            if first:
                idx2 = load_list(offs2, "idx2")
            page = sbuf([P, T2], F32, "page%d" % i)
            nc.sync.dma_start(page[:], page_rows[b, t])
            if first:
                for half in range(HALVES):
                    load_wgs(t, slice(half * BANK, (half + 1) * BANK))
                idx4 = load_list(offs4, "idx4")
                idx3 = load_list(offs3, "idx3")
            elif b == 0:
                load_wgs(t, slice(0, S))
            if i == w1_after - 1:
                w1_raw.append(load_w1(1))

            h = sbuf([P, S], F32, "h%d" % i, "h%d" % (i % H_BUFS))
            for half in range(HALVES):
                if first:
                    features_first(half, y, h)
                else:
                    features(i, half, y, h)

            if i == vectors_after:
                x2_sb = turn_vectors(x2_vectors, "x2_vectors", y_tag)
            if i == w1_after:
                w1q.append(quantize_w1(1, y_tag))
            if i == x1_after:
                woven = sbuf([P, P2 * PACK], BF16, "x1_woven0", y_tag)
                x1q.append(
                    quantize(weave(woven[:], x1_places[0], 0, PACK), "x1q0", "wgs%d" % (t - 1))
                )
            if i == x2_after:
                woven = sbuf([P, P2 * PACK], BF16, "x2_woven0", y_tag)
                x2q.append(
                    quantize(weave(woven[:], x2_places[0], 0, PACK), "x2q0", "wgs%d" % (t - 1))
                )
            if last:
                woven = sbuf([P, 2 * P2 * PACK], BF16, "woven1", "tanh_sb1")
                x2_last = weave(woven[:, P2 * PACK :], x2_places[b], 0, PACK - 1)
                x1_last = weave(woven[:, : P2 * PACK], x1_places[b], 0, PACK - 1)

            width = BANK if first else S
            for j0 in range(0, S, width):
                nc.vector.tensor_tensor(
                    page[:].indirect(idx2[:, j0 // STRIPE : (j0 + width) // STRIPE]),
                    h[:, j0 : j0 + width], wgs_sb[t][:, j0 : j0 + width], ALU.mult,
                )

            if last:
                nc.vector.tensor_copy(x1_places[b][:, t, :], page[:].indirect(idx3[:]))
                weave(x1_last, x1_places[b], t, 1)
                x2_raw = sbuf([P, P2], F32, "x2_raw", "x2_places%d" % b)
                x2_out = x2_last.rearrange("p (c t) -> p t c", t=PACK)[:, t, :]
                nc.vector.tensor_copy(x2_raw[:], page[:].indirect(idx4[:]))
            else:
                x2_raw = sbuf([P, P2], F32, "x2_raw", "x2_raw%d" % (i % 2))
                x2_out = x2_places[b][:, t, :]
                nc.vector.tensor_copy(x2_raw[:], page[:].indirect(idx4[:]))
                nc.vector.tensor_copy(x1_places[b][:, t, :], page[:].indirect(idx3[:]))
            nc.vector.tensor_scalar(
                x2_out, x2_raw[:], x2_sb[:, t, b : b + 1], x2_sb[:, t, GROUPS + b : GROUPS + b + 1],
                ALU.max, ALU.mult,
            )

        gel_sb = sbuf([P, P2 // P], F32, "gel_sb")
        with nc.allow_non_contiguous_dma(reason="one gel factor for each partition"):
            nc.sync.dma_start(gel_sb[:], gel.rearrange("(c p) -> p c", p=P))
        tmpl_sb = sbuf([P, P2], F32, "tmpl_sb")
        nc.sync.dma_start(tmpl_sb[:], tmpl.partition_broadcast(P))

        x1_codes = sbuf([P, P2], U32, "x1q1_codes")
        x1_plane = sbuf([P, P2], U8, "x1q1_plane")
        nc.vector.quantize_mx(
            out=x1_codes[:, :P].bitcast(FP8X4), scales=x1_plane[:, :P], in_=x1_last[:, : P * PACK]
        )
        x2q.append(quantize(x2_last, "x2q1"))
        nc.vector.quantize_mx(
            out=x1_codes[:, P:].bitcast(FP8X4), scales=x1_plane[:, P:], in_=x1_last[:, P * PACK :]
        )
        x1q.append((x1_codes, x1_plane))

        for c, bank in enumerate(("back0", "back1", "sum0", "sum1")):
            e_ps = psum.tile([P, P2], F32, name="e_ps", tag=bank)
            for b in range(GROUPS):
                nc.tensor.matmul_mx(
                    e_ps[:], lhsT=x1q[b][0][:, c * P : (c + 1) * P].bitcast(FP8X4),
                    lhsT_scale=x1q[b][1][:, c * P : (c + 1) * P],
                    rhs=x2q[b][0][:].bitcast(FP8X4), rhs_scale=x2q[b][1][:],
                    start=(b == 0), stop=(b == GROUPS - 1),
                )
            result = sbuf([P, P2], F32, "result%d" % c)
            nc.vector.scalar_tensor_tensor(
                result[:], e_ps[:], gel_sb[:, c : c + 1], tmpl_sb[:], ALU.mult, ALU.add
            )
            nc.sync.dma_start(out[c * P : (c + 1) * P, :], result[:])
